import numpy as np
import ml_dtypes


def mxq(x, axis, fmt="e4m3"):
    dtype, down = {"e4m3": (ml_dtypes.float8_e4m3fn, 7), "e5m2": (ml_dtypes.float8_e5m2, 14)}[fmt]
    v = np.moveaxis(np.asarray(x, np.float32).astype(ml_dtypes.bfloat16).astype(np.float64), axis, -1)
    blocks = v.reshape(v.shape[:-1] + (-1, 32))
    amax = np.abs(blocks).max(-1, keepdims=True)
    byte = np.maximum(np.where(amax > 0, np.frexp(amax)[1] - 1 + 127, 0) - down, 1)
    scale = np.exp2(byte - 127.0)
    codes = (blocks / scale).astype(np.float32).astype(dtype).astype(np.float64)
    return np.moveaxis((codes * scale).reshape(v.shape), -1, axis)


WIDE = False


def mx_kscale(k):
    if not WIDE:
        return np.ones(k)
    levels = np.array([10, -10, 5, -5, 0])
    if k % 512:
        return np.exp2(np.random.permutation(np.resize(levels, k // 32))).repeat(32)
    a = np.empty((k // 512, 16))
    for p in range(k // 512):
        a[p, :8] = np.random.permutation(np.resize(levels, 8))
        for g in range(8):
            far = levels[np.abs(levels - a[p, g]) >= 10]
            a[p, g + 8] = far[np.random.randint(len(far))]
    return np.exp2(a.ravel()).repeat(32)


BF16 = ml_dtypes.bfloat16


def bf(x):
    return np.asarray(x, np.float32).astype(BF16)


def f64(x):
    return np.asarray(x).astype(np.float64)


E2M1 = np.array([0.0, 0.5, 1.0, 1.5, 2.0, 3.0, 4.0, 6.0, -0.0, -0.5, -1.0, -1.5, -2.0, -3.0, -4.0, -6.0])


def pack_weight(w, fmt):
    k, n = w.shape
    w = f64(bf(w)).reshape(k // 32, 32, n)
    amax = np.abs(w).max(1)
    if fmt == "e4m3":
        byte = np.frexp(amax)[1] - 1 + 127 - 7
    else:
        mant, ex = np.frexp(amax / 6.0)
        byte = np.where(mant > 0.5, ex, ex - 1) + 127
    byte = np.clip(np.where(amax > 0, byte, 1), 1, 254)
    scaled = (w * np.exp2(127.0 - byte)[:, None, :]).reshape(k, n).astype(np.float32)
    by_word = np.ascontiguousarray(scaled.reshape(k // 512, 128, 4, n).transpose(0, 1, 3, 2))
    if fmt == "e4m3":
        words = by_word.astype(ml_dtypes.float8_e4m3fn).view(np.uint8)
    else:
        c = by_word.astype(ml_dtypes.float4_e2m1fn).view(np.uint8) & 0xF
        words = c[..., 0::2] | (c[..., 1::2] << 4)
    return np.ascontiguousarray(words), np.ascontiguousarray(byte.astype(np.uint8).reshape(k // 512, 16, n))


def unpack_weight(words, scales, fmt):
    g, p, n, _ = words.shape
    if fmt == "e4m3":
        vals = np.ascontiguousarray(words).view(ml_dtypes.float8_e4m3fn).astype(np.float64)
    else:
        nib = np.empty((g, p, n, 4), np.uint8)
        nib[..., 0::2] = words & 0xF
        nib[..., 1::2] = words >> 4
        vals = E2M1[nib]
    vals = vals * np.repeat(np.exp2(scales.astype(np.float64) - 127.0), 8, axis=1)[..., None]
    return vals.transpose(0, 1, 3, 2).reshape(g * 512, n)
def pack4(w):
    words, scales = pack_weight(w, "e2m1")
    return words.reshape(words.shape[0], 128, -1), scales


def unpack4(words, scales):
    return unpack_weight(words.reshape(words.shape[0], 128, -1, 2), scales, "e2m1")


def planes(Y):
    n, m = Y.shape
    b = f64(bf(Y)).reshape(n // 32, 32, m)
    amax = np.abs(b).max(1)
    byte = np.clip(np.where(amax > 0, np.frexp(amax)[1] - 1 + 127 - 7, 1), 1, 254)
    codes = (b * np.exp2(127.0 - byte)[:, None, :]).reshape(n, m).astype(np.float32).astype(ml_dtypes.float8_e4m3fn).view(np.uint8)
    words = codes.reshape(n // 512, 128, 4, m).transpose(0, 1, 3, 2)
    return np.ascontiguousarray(words), np.ascontiguousarray(byte.astype(np.uint8).reshape(n // 512, 16, m))


U, D, N = 768, 1536, 1024


def setup_inputs():
    s = mx_kscale(D)
    x_words, x_scales = pack_weight(np.random.randn(D, U) * s[:, None], "e4m3")
    w_a = np.random.randn(D, N) / np.sqrt(D) / s[:, None]
    w_b = np.random.randn(D, N) / np.sqrt(D) / s[:, None]
    return {
        "x_words": x_words,
        "x_scales": x_scales,
        "w_a": bf(w_a),
        "b_a": bf(0.4 * np.random.randn(N)),
        "w_b": bf(w_b),
        "b_b": bf(0.4 * np.random.randn(N)),
        "c": bf(np.exp(0.8 * np.random.randn(N))),
    }


def reference(x_words, x_scales, w_a, b_a, w_b, b_b, c):
    X = unpack_weight(x_words, x_scales, "e4m3")
    a = (X.T @ mxq(f64(w_a), 0, "e4m3")) + f64(b_a)
    b = (X.T @ mxq(f64(w_b), 0, "e4m3")) + f64(b_b)
    y = a * b * f64(c)
    Y = y.T
    words, scales = planes(Y)
    return y, words, scales

@@ -1,0 +1,326 @@
+from contextlib import ExitStack
+
+import concourse.mybir as mybir
+from concourse.masks import make_identity
+
+U, D, N = 768, 1536, 1024
+FLOPS = 2 * 2 * U * D * N
+
+F32 = mybir.dt.float32
+BF16 = mybir.dt.bfloat16
+I32 = mybir.dt.int32
+U32 = mybir.dt.uint32
+U8 = mybir.dt.uint8
+FP8X4 = mybir.dt.float8_e4m3fn_x4
+ACT = mybir.ActivationFunctionType
+ALU = mybir.AluOpType
+
+P = 128
+PACK = 4
+GROUP = P * PACK
+K_GROUPS = D // GROUP
+N_GROUPS = N // GROUP
+WIDE, NARROW = 512, 256
+CHUNKS = ((0, WIDE), (WIDE, NARROW))
+PAIRS = P // 2
+
+V_SHARE = (40, 36, 36, 56, 64, 44, 8, 0, 24, 48, 64, 52)
+
+
+def tile_multiplied_user_latents_g6_kernel(
+    tc, x_words, x_scales, w_a, b_a, w_b, b_b, c, out_0, out_1, out_2
+):
+    nc = tc.nc
+    weights = (w_a, w_b)
+
+    with ExitStack() as ctx:
+        keep = ctx.enter_context(tc.tile_pool(name="keep", bufs=1))
+        stage = ctx.enter_context(tc.tile_pool(name="stage", bufs=4))
+        psum = ctx.enter_context(tc.psum_pool(name="psum", bufs=1))
+        ctx.enter_context(tc.manual_schedule())
+
+        pieces = [(h, w, g) for h in range(N_GROUPS) for w in range(2) for g in range(K_GROUPS)]
+
+        raw = [keep.tile([P, PACK, GROUP], BF16, name="raw%d" % i, align_bytes=64) for i in range(len(pieces))]
+        w_codes = [keep.tile([P, GROUP], U32, name="w_codes%d" % i, align_bytes=64) for i in range(len(pieces))]
+        w_planes = [keep.tile([P, GROUP], U8, name="w_planes%d" % i, align_bytes=64) for i in range(len(pieces))]
+        x_codes = [keep.tile([P, U], U32, name="x_codes%d" % g, align_bytes=64) for g in range(K_GROUPS)]
+        x_plane = keep.tile([P, K_GROUPS * U], U8, name="x_plane", align_bytes=64)
+        ba_sb = keep.tile([P, N_GROUPS * PACK], BF16, name="ba_sb")
+        bb_sb = keep.tile([P, N_GROUPS * PACK], BF16, name="bb_sb")
+        c_sb = keep.tile([P, N_GROUPS * PACK], BF16, name="c_sb")
+        c32 = keep.tile([P, N_GROUPS * PACK], F32, name="c32")
+        bac = keep.tile([P, N_GROUPS * PACK], F32, name="bac")
+        ident = keep.tile([P, P], F32, name="ident")
+
+        x_i32 = x_words.rearrange("g p u t -> g p (u t)").bitcast(I32)
+        xs_i32 = x_scales.bitcast(I32)
+        codes_out = out_1.rearrange("g p u t -> g p (u t)").bitcast(I32)
+        planes_out = out_2.bitcast(I32)
+
+        def load_piece(i):
+            h, w, g = pieces[i]
+            rows = weights[w][g * GROUP : (g + 1) * GROUP, h * GROUP : (h + 1) * GROUP]
+            nc.sync.dma_start(out=raw[i][:], in_=rows.rearrange("(p j) n -> p j n", j=PACK))
+
+        def load_vec(queue, dst, vec):
+            queue.dma_start(
+                out=dst[:].rearrange("p (h t) -> p h t", t=PACK),
+                in_=vec.rearrange("(h p t) -> p h t", p=P, t=PACK),
+            )
+
+        grouped = {}
+
+        def interleave(i, on_vector):
+            if i not in grouped:
+                grouped[i] = stage.tile([P, GROUP * PACK], BF16, name="grouped", align_bytes=64)
+            lo, hi = (0, V_SHARE[i]) if on_vector else (V_SHARE[i], PAIRS)
+            if lo == hi:
+                return
+            dst = grouped[i][:].rearrange("p (t q m j) -> p q t m j", t=PACK, m=2, j=PACK)[:, lo:hi]
+            src = raw[i][:].rearrange("p j (q m t) -> p q t m j", m=2, t=PACK)[:, lo:hi]
+            if on_vector:
+                nc.vector.tensor_copy(out=dst, in_=src)
+            else:
+                nc.scalar.copy(out=dst, in_=src)
+
+        def quantize_piece(i):
+            nc.vector.quantize_mx(out=w_codes[i][:].bitcast(FP8X4), scales=w_planes[i][:], in_=grouped[i][:])
+
+        def mx_pass(acc, i, t, chunk):
+            g = pieces[i][2]
+            u0, width = CHUNKS[chunk]
+            cols = slice(t * P, (t + 1) * P)
+            nc.tensor.matmul_mx(
+                out=acc,
+                lhsT=w_codes[i][:, cols].bitcast(FP8X4),
+                lhsT_scale=w_planes[i][:, cols],
+                rhs=x_codes[g][:, u0 : u0 + width].bitcast(FP8X4),
+                rhs_scale=x_plane[:, g * U + u0 : g * U + u0 + width],
+                start=(g == 0),
+                stop=(g == K_GROUPS - 1),
+            )
+
+        sums = {}
+
+        def take_bank(b):
+            return psum.tile([P, WIDE], F32, name="bank%d" % b)
+
+        def mm(i, chunk, banks=None):
+            h, w, g = pieces[i]
+            for t in range(PACK):
+                if g == 0:
+                    sums[h, w, chunk, t] = take_bank(banks[t])[:, 0 : CHUNKS[chunk][1]]
+                mx_pass(sums[h, w, chunk, t], i, t, chunk)
+
+        def mm_both(i, banks=None):
+            h, w, g = pieces[i]
+            for t in range(PACK):
+                for chunk in (1, 0):
+                    if g == 0:
+                        sums[h, w, chunk, t] = take_bank(banks[chunk][t])[:, 0 : CHUNKS[chunk][1]]
+                    mx_pass(sums[h, w, chunk, t], i, t, chunk)
+
+        def mm_narrow(h, w, banks):
+            first = pieces.index((h, w, 0))
+            for t in range(PACK):
+                if t % 2 == 0:
+                    bank = take_bank(banks[t // 2])
+                sums[h, w, 1, t] = bank[:, (t % 2) * NARROW : (t % 2 + 1) * NARROW]
+                for g in range(K_GROUPS):
+                    mx_pass(sums[h, w, 1, t], first + g, t, 1)
+
+        scaled = {}
+        y_t = {}
+
+        for h in range(N_GROUPS):
+            for chunk in range(2):
+                width = CHUNKS[chunk][1]
+                scaled[h, chunk] = keep.tile([P, PACK * width], F32, name="scaled%d_%d" % (h, chunk))
+                y_t[h, chunk] = keep.tile([P, PACK * width], F32, name="y_t%d_%d" % (h, chunk))
+
+        def scale_a(h, chunk, t):
+            width = CHUNKS[chunk][1]
+            col = slice(h * PACK + t, h * PACK + t + 1)
+            nc.scalar.activation(
+                out=scaled[h, chunk][:, t * width : (t + 1) * width],
+                in_=sums[h, 0, chunk, t],
+                func=ACT.Identity,
+                scale=c32[:, col],
+                bias=bac[:, col],
+            )
+
+        def multiply(h, chunk, t, lo=0, hi=None):
+            width = CHUNKS[chunk][1]
+            hi = hi or width
+            col = slice(h * PACK + t, h * PACK + t + 1)
+            nc.vector.scalar_tensor_tensor(
+                out=y_t[h, chunk][:, t * width + lo : t * width + hi],
+                in0=sums[h, 1, chunk, t][:, lo:hi],
+                scalar=bb_sb[:, col],
+                in1=scaled[h, chunk][:, t * width + lo : t * width + hi],
+                op0=ALU.add,
+                op1=ALU.mult,
+            )
+
+        turned = {}
+
+        def turn(h, ut, b):
+            chunk = 0 if ut * P < WIDE else 1
+            u0, width = CHUNKS[chunk]
+            bank = take_bank(b)
+            turned[h, ut] = bank
+            for t in range(PACK):
+                at = t * width + ut * P - u0
+                nc.tensor.transpose(bank[:, t * P : (t + 1) * P], y_t[h, chunk][:, at : at + P], ident[:])
+
+        def store_y(h, first, count):
+            y_sb = keep.tile([P, count, GROUP], F32, name="y_sb%d_%d" % (h, first))
+            for e in range(count):
+                nc.scalar.copy(
+                    out=y_sb[:, e, :].rearrange("u (m t) -> u m t", t=PACK),
+                    in_=turned[h, first + e][:].rearrange("u (t m) -> u m t", t=PACK),
+                )
+            rows = out_0[first * P : (first + count) * P, h * GROUP : (h + 1) * GROUP]
+            nc.sync.dma_start(out=rows.rearrange("(e u) n -> u e n", e=count), in_=y_sb[:])
+
+        y_bf = {}
+        y_codes = [keep.tile([P, U], U32, name="y_codes%d" % h, align_bytes=64) for h in range(N_GROUPS)]
+        y_plane = [keep.tile([P, U], U8, name="y_plane%d" % h, align_bytes=64) for h in range(N_GROUPS)]
+
+        def round_y(h, chunk, on_vector=True):
+            width = CHUNKS[chunk][1]
+            y_bf[h, chunk] = keep.tile([P, PACK * width], BF16, name="y_bf%d_%d" % (h, chunk), align_bytes=64)
+            dst = y_bf[h, chunk][:].rearrange("p (u t) -> p u t", t=PACK)
+            src = y_t[h, chunk][:].rearrange("p (t u) -> p u t", t=PACK)
+            if on_vector:
+                nc.vector.tensor_copy(out=dst, in_=src)
+            else:
+                nc.scalar.copy(out=dst, in_=src)
+
+        def quantize_y(h, chunk):
+            u0, width = CHUNKS[chunk]
+            cols = slice(u0, u0 + width)
+            nc.vector.quantize_mx(out=y_codes[h][:, cols].bitcast(FP8X4), scales=y_plane[h][:, cols], in_=y_bf[h, chunk][:])
+            nc.sync.dma_start(out=codes_out[h, :, cols], in_=y_codes[h][:, cols].bitcast(I32))
+
+        def store_planes(h):
+            for q in range(4):
+                nc.sync.dma_start(
+                    out=planes_out[h, 4 * q : 4 * q + 4, :], in_=y_plane[h][32 * q : 32 * q + 4, :].bitcast(I32)
+                )
+
+        nc.gpsimd.memset(x_plane[:].bitcast(I32), 0)
+        make_identity(nc, ident[:])
+        load_vec(nc.scalar, c_sb, c)
+        load_piece(0)
+        nc.sync.dma_start(out=x_codes[0][:].bitcast(I32), in_=x_i32[0])
+        for q in range(4):
+            nc.sync.dma_start(
+                out=x_plane[32 * q : 32 * q + 4, :].bitcast(I32).rearrange("r (g u) -> r g u", g=K_GROUPS),
+                in_=xs_i32[:, 4 * q : 4 * q + 4, :].rearrange("g r u -> r g u"),
+            )
+        for g in range(1, K_GROUPS):
+            load_piece(g)
+            nc.sync.dma_start(out=x_codes[g][:].bitcast(I32), in_=x_i32[g])
+        load_vec(nc.sync, ba_sb, b_a)
+        load_vec(nc.sync, bb_sb, b_b)
+        for i in range(K_GROUPS, len(pieces)):
+            load_piece(i)
+
+        nc.scalar.activation(out=c32[:], in_=c_sb[:], func=ACT.Identity)
+
+        def both(i):
+            interleave(i, True)
+            interleave(i, False)
+
+        LO, HI = (0, 1, 2, 3), (4, 5, 6, 7)
+        for i in range(3):
+            both(i)
+            quantize_piece(i)
+            mm_both(i, (LO, HI))
+        nc.vector.tensor_tensor(out=bac[:], in0=ba_sb[:], in1=c_sb[:], op=ALU.mult)
+        both(3)
+        for t in range(PACK):
+            scale_a(0, 1, t)
+            scale_a(0, 0, t)
+        quantize_piece(3)
+        mm_both(3, (LO, HI))
+        both(4)
+        quantize_piece(4)
+        mm_both(4)
+        both(5)
+        quantize_piece(5)
+        mm(5, 1)
+        mm(5, 0)
+        both(6)
+        multiply(0, 1, 0)
+        multiply(0, 1, 1)
+        quantize_piece(6)
+        multiply(0, 1, 2)
+        multiply(0, 1, 3)
+        mm(6, 0, HI)
+        multiply(0, 0, 0)
+        multiply(0, 0, 1)
+        both(7)
+        multiply(0, 0, 2)
+        quantize_piece(7)
+        multiply(0, 0, 3)
+        turn(0, 4, 0)
+        turn(0, 5, 1)
+        mm(7, 0)
+        both(8)
+        store_y(0, 4, 2)
+        quantize_piece(8)
+        turn(0, 0, 2)
+        turn(0, 1, 3)
+        mm(8, 0)
+        both(9)
+        store_y(0, 0, 2)
+        turn(0, 2, 0)
+        turn(0, 3, 1)
+        mm_narrow(1, 0, (2, 3))
+        round_y(0, 1)
+        quantize_piece(9)
+        for t in range(PACK):
+            scale_a(1, 0, t)
+        mm(9, 0, HI)
+        interleave(10, True)
+        quantize_y(0, 1)
+        store_y(0, 2, 2)
+        interleave(10, False)
+        quantize_piece(10)
+        mm(10, 0)
+        interleave(11, True)
+        for t in range(PACK):
+            scale_a(1, 1, t)
+        interleave(11, False)
+        mm(9, 1, LO)
+        mm(10, 1)
+        quantize_piece(11)
+        mm(11, 1)
+        mm(11, 0)
+        round_y(0, 0, False)
+        for t in range(PACK):
+            multiply(1, 1, t)
+        turn(1, 4, 0)
+        turn(1, 5, 1)
+        for t in range(PACK):
+            multiply(1, 0, t, 0, NARROW)
+        store_y(1, 4, 1)
+        store_y(1, 5, 1)
+        turn(1, 0, 2)
+        turn(1, 1, 3)
+        for t in range(PACK):
+            multiply(1, 0, t, NARROW, WIDE)
+        store_y(1, 0, 2)
+        turn(1, 2, 0)
+        turn(1, 3, 1)
+        round_y(1, 1)
+        quantize_y(0, 0)
+        store_planes(0)
+        store_y(1, 2, 2)
+        round_y(1, 0)
+        quantize_y(1, 1)
+        quantize_y(1, 0)
+        store_planes(1)

@@ -24,7 +24,8 @@ WIDE, NARROW = 512, 256
 CHUNKS = ((0, WIDE), (WIDE, NARROW))
 PAIRS = P // 2
 
-V_SHARE = (40, 36, 36, 56, 64, 44, 8, 0, 24, 48, 64, 52)
+V_SHARE = (40, 40, 40, 64, 64, 40, 20, 0, 0, 64, 64, 20)
+LOADS = (("w", 1), ("x", 1), ("w", 2), ("x", 2), ("b", 0), ("w", 3), ("w", 4), ("w", 5), ("w", 6), ("w", 7), ("w", 8), ("w", 9), ("w", 10), ("w", 11))
 
 
 def tile_multiplied_user_latents_g6_kernel(
@@ -74,18 +75,25 @@ def tile_multiplied_user_latents_g6_kernel(
         def interleave(i, on_vector):
             if i not in grouped:
                 grouped[i] = stage.tile([P, GROUP * PACK], BF16, name="grouped", align_bytes=64)
-            lo, hi = (0, V_SHARE[i]) if on_vector else (V_SHARE[i], PAIRS)
-            if lo == hi:
-                return
-            dst = grouped[i][:].rearrange("p (t q m j) -> p q t m j", t=PACK, m=2, j=PACK)[:, lo:hi]
-            src = raw[i][:].rearrange("p j (q m t) -> p q t m j", m=2, t=PACK)[:, lo:hi]
-            if on_vector:
-                nc.vector.tensor_copy(out=dst, in_=src)
-            else:
-                nc.scalar.copy(out=dst, in_=src)
+            dst = grouped[i][:].rearrange("p (s t q m j) -> p s q j t m", s=2, t=2, m=2, j=PACK)
+            src = raw[i][:].rearrange("p j (q m s t) -> p s q j t m", m=2, s=2, t=2)
+            for s in range(2):
+                cut = min(max(V_SHARE[i] * 2 - s * PAIRS, 0), PAIRS)
+                lo, hi = (0, cut) if on_vector else (cut, PAIRS)
+                if lo < hi:
+                    if on_vector:
+                        nc.vector.tensor_copy(out=dst[:, s, lo:hi], in_=src[:, s, lo:hi])
+                    else:
+                        nc.scalar.copy(out=dst[:, s, lo:hi], in_=src[:, s, lo:hi])
 
-        def quantize_piece(i):
-            nc.vector.quantize_mx(out=w_codes[i][:].bitcast(FP8X4), scales=w_planes[i][:], in_=grouped[i][:])
+        def quantize_piece(i, halves=(0, 1)):
+            for s in halves:
+                cols = slice(s * 2 * P, (s + 1) * 2 * P)
+                nc.vector.quantize_mx(
+                    out=w_codes[i][:, cols].bitcast(FP8X4),
+                    scales=w_planes[i][:, cols],
+                    in_=grouped[i][:, s * 2 * GROUP : (s + 1) * 2 * GROUP],
+                )
 
         def mx_pass(acc, i, t, chunk):
             g = pieces[i][2]
@@ -121,12 +129,12 @@ def tile_multiplied_user_latents_g6_kernel(
                         sums[h, w, chunk, t] = take_bank(banks[chunk][t])[:, 0 : CHUNKS[chunk][1]]
                     mx_pass(sums[h, w, chunk, t], i, t, chunk)
 
-        def mm_narrow(h, w, banks):
+        def mm_narrow(h, w, pair, b):
             first = pieces.index((h, w, 0))
-            for t in range(PACK):
-                if t % 2 == 0:
-                    bank = take_bank(banks[t // 2])
-                sums[h, w, 1, t] = bank[:, (t % 2) * NARROW : (t % 2 + 1) * NARROW]
+            bank = take_bank(b)
+            for e in range(2):
+                t = 2 * pair + e
+                sums[h, w, 1, t] = bank[:, e * NARROW : (e + 1) * NARROW]
                 for g in range(K_GROUPS):
                     mx_pass(sums[h, w, 1, t], first + g, t, 1)
 
@@ -186,13 +194,13 @@ def tile_multiplied_user_latents_g6_kernel(
 
         y_bf = {}
         y_codes = [keep.tile([P, U], U32, name="y_codes%d" % h, align_bytes=64) for h in range(N_GROUPS)]
-        y_plane = [keep.tile([P, U], U8, name="y_plane%d" % h, align_bytes=64) for h in range(N_GROUPS)]
+        y_planes = keep.tile([P, U], U8, name="y_planes", align_bytes=64)
 
         def round_y(h, chunk, on_vector=True):
             width = CHUNKS[chunk][1]
             y_bf[h, chunk] = keep.tile([P, PACK * width], BF16, name="y_bf%d_%d" % (h, chunk), align_bytes=64)
-            dst = y_bf[h, chunk][:].rearrange("p (u t) -> p u t", t=PACK)
-            src = y_t[h, chunk][:].rearrange("p (t u) -> p u t", t=PACK)
+            dst = y_bf[h, chunk][:].rearrange("p (v e t) -> p v t e", t=PACK, e=PACK)
+            src = y_t[h, chunk][:].rearrange("p (t v e) -> p v t e", t=PACK, e=PACK)
             if on_vector:
                 nc.vector.tensor_copy(out=dst, in_=src)
             else:
@@ -201,13 +209,15 @@ def tile_multiplied_user_latents_g6_kernel(
         def quantize_y(h, chunk):
             u0, width = CHUNKS[chunk]
             cols = slice(u0, u0 + width)
-            nc.vector.quantize_mx(out=y_codes[h][:, cols].bitcast(FP8X4), scales=y_plane[h][:, cols], in_=y_bf[h, chunk][:])
+            nc.vector.quantize_mx(out=y_codes[h][:, cols].bitcast(FP8X4), scales=y_planes[4 * h :, cols], in_=y_bf[h, chunk][:])
             nc.sync.dma_start(out=codes_out[h, :, cols], in_=y_codes[h][:, cols].bitcast(I32))
 
-        def store_planes(h):
+        def store_planes():
             for q in range(4):
-                nc.sync.dma_start(
-                    out=planes_out[h, 4 * q : 4 * q + 4, :], in_=y_plane[h][32 * q : 32 * q + 4, :].bitcast(I32)
+                queue = nc.sync if q % 2 == 0 else nc.scalar
+                queue.dma_start(
+                    out=planes_out[:, 4 * q : 4 * q + 4, :],
+                    in_=y_planes[32 * q : 32 * q + 4 * N_GROUPS, :].bitcast(I32),
                 )
 
         nc.gpsimd.memset(x_plane[:].bitcast(I32), 0)
@@ -220,13 +230,14 @@ def tile_multiplied_user_latents_g6_kernel(
                 out=x_plane[32 * q : 32 * q + 4, :].bitcast(I32).rearrange("r (g u) -> r g u", g=K_GROUPS),
                 in_=xs_i32[:, 4 * q : 4 * q + 4, :].rearrange("g r u -> r g u"),
             )
-        for g in range(1, K_GROUPS):
-            load_piece(g)
-            nc.sync.dma_start(out=x_codes[g][:].bitcast(I32), in_=x_i32[g])
-        load_vec(nc.sync, ba_sb, b_a)
-        load_vec(nc.sync, bb_sb, b_b)
-        for i in range(K_GROUPS, len(pieces)):
-            load_piece(i)
+        for kind, n in LOADS:
+            if kind == "w":
+                load_piece(n)
+            elif kind == "x":
+                nc.sync.dma_start(out=x_codes[n][:].bitcast(I32), in_=x_i32[n])
+            else:
+                load_vec(nc.sync, ba_sb, b_a)
+                load_vec(nc.sync, bb_sb, b_b)
 
         nc.scalar.activation(out=c32[:], in_=c_sb[:], func=ACT.Identity)
 
@@ -263,64 +274,64 @@ def tile_multiplied_user_latents_g6_kernel(
         multiply(0, 0, 0)
         multiply(0, 0, 1)
         both(7)
-        multiply(0, 0, 2)
         quantize_piece(7)
+        multiply(0, 0, 2)
         multiply(0, 0, 3)
         turn(0, 4, 0)
         turn(0, 5, 1)
         mm(7, 0)
         both(8)
-        store_y(0, 4, 2)
         quantize_piece(8)
-        turn(0, 0, 2)
-        turn(0, 1, 3)
         mm(8, 0)
-        both(9)
-        store_y(0, 0, 2)
-        turn(0, 2, 0)
-        turn(0, 3, 1)
-        mm_narrow(1, 0, (2, 3))
-        round_y(0, 1)
-        quantize_piece(9)
+        mm_narrow(1, 0, 0, 2)
+        mm_narrow(1, 0, 1, 3)
+        store_y(0, 4, 2)
+        interleave(9, True)
         for t in range(PACK):
             scale_a(1, 0, t)
+        interleave(9, False)
+        quantize_piece(9)
+        turn(0, 0, 0)
+        turn(0, 1, 1)
         mm(9, 0, HI)
         interleave(10, True)
-        quantize_y(0, 1)
-        store_y(0, 2, 2)
+        round_y(0, 0)
+        for t in range(PACK):
+            scale_a(1, 1, t)
         interleave(10, False)
         quantize_piece(10)
         mm(10, 0)
-        interleave(11, True)
-        for t in range(PACK):
-            scale_a(1, 1, t)
-        interleave(11, False)
-        mm(9, 1, LO)
-        mm(10, 1)
+        turn(0, 2, 2)
+        turn(0, 3, 3)
+        both(11)
+        quantize_y(0, 0)
         quantize_piece(11)
-        mm(11, 1)
         mm(11, 0)
-        round_y(0, 0, False)
-        for t in range(PACK):
-            multiply(1, 1, t)
-        turn(1, 4, 0)
-        turn(1, 5, 1)
+        store_y(0, 0, 2)
+        store_y(0, 2, 2)
+        mm_narrow(1, 1, 0, 0)
         for t in range(PACK):
             multiply(1, 0, t, 0, NARROW)
-        store_y(1, 4, 1)
-        store_y(1, 5, 1)
         turn(1, 0, 2)
         turn(1, 1, 3)
+        round_y(0, 1, False)
         for t in range(PACK):
             multiply(1, 0, t, NARROW, WIDE)
         store_y(1, 0, 2)
-        turn(1, 2, 0)
-        turn(1, 3, 1)
-        round_y(1, 1)
-        quantize_y(0, 0)
-        store_planes(0)
-        store_y(1, 2, 2)
+        turn(1, 2, 4)
+        turn(1, 3, 5)
+        mm_narrow(1, 1, 1, 1)
+        multiply(1, 1, 0)
+        multiply(1, 1, 1)
         round_y(1, 0)
-        quantize_y(1, 1)
+        store_y(1, 2, 2)
+        multiply(1, 1, 2)
+        multiply(1, 1, 3)
+        turn(1, 4, 6)
+        turn(1, 5, 7)
+        quantize_y(0, 1)
         quantize_y(1, 0)
-        store_planes(1)
+        store_y(1, 4, 2)
+        round_y(1, 1)
+        quantize_y(1, 1)
+        store_planes()

@@ -19,13 +19,22 @@ P = 128
 PACK = 4
 GROUP = P * PACK
 K_GROUPS = D // GROUP
-N_GROUPS = N // GROUP
-WIDE, NARROW = 512, 256
-CHUNKS = ((0, WIDE), (WIDE, NARROW))
-PAIRS = P // 2
+HALVES = N // GROUP
+BANK = 512
+QUADRANT = 32
+LIVE_ROWS = 4
+A, B = 0, 1
 
-V_SHARE = (40, 40, 40, 64, 64, 40, 20, 0, 0, 64, 64, 20)
-LOADS = (("w", 1), ("x", 1), ("w", 2), ("x", 2), ("b", 0), ("w", 3), ("w", 4), ("w", 5), ("w", 6), ("w", 7), ("w", 8), ("w", 9), ("w", 10), ("w", 11))
+WIDE, NARROW = 0, 1
+CHUNKS = ((0, BANK), (BANK, U - BANK))
+
+STRIPS = 128
+BOTH_FREE = 80
+VECTOR_ALONE = STRIPS
+SCALAR_ALONE = 0
+BEFORE_PRODUCT = 64
+LAST_BUT_ONE = 112
+LAST = 48
 
 
 def tile_multiplied_user_latents_g6_kernel(
@@ -40,298 +49,296 @@ def tile_multiplied_user_latents_g6_kernel(
         psum = ctx.enter_context(tc.psum_pool(name="psum", bufs=1))
         ctx.enter_context(tc.manual_schedule())
 
-        pieces = [(h, w, g) for h in range(N_GROUPS) for w in range(2) for g in range(K_GROUPS)]
-
-        raw = [keep.tile([P, PACK, GROUP], BF16, name="raw%d" % i, align_bytes=64) for i in range(len(pieces))]
-        w_codes = [keep.tile([P, GROUP], U32, name="w_codes%d" % i, align_bytes=64) for i in range(len(pieces))]
-        w_planes = [keep.tile([P, GROUP], U8, name="w_planes%d" % i, align_bytes=64) for i in range(len(pieces))]
-        x_codes = [keep.tile([P, U], U32, name="x_codes%d" % g, align_bytes=64) for g in range(K_GROUPS)]
+        pieces = [(h, w, g) for h in range(HALVES) for w in (A, B) for g in range(K_GROUPS)]
+        raw, w_codes, w_plane = {}, {}, {}
+        for piece in pieces:
+            raw[piece] = keep.tile([P, PACK, GROUP], BF16, name="raw%d%d%d" % piece, align_bytes=64)
+        for piece in pieces:
+            w_codes[piece] = keep.tile([P, GROUP], U32, name="w_codes%d%d%d" % piece, align_bytes=64)
+        for piece in pieces:
+            w_plane[piece] = keep.tile([P, GROUP], U8, name="w_plane%d%d%d" % piece, align_bytes=64)
+        narrow_users = CHUNKS[NARROW][1]
+        x_wide = [keep.tile([P, BANK], U32, name="x_wide%d" % g, align_bytes=64) for g in range(K_GROUPS)]
+        x_narrow = keep.tile([P, K_GROUPS * narrow_users], U32, name="x_narrow", align_bytes=64)
         x_plane = keep.tile([P, K_GROUPS * U], U8, name="x_plane", align_bytes=64)
-        ba_sb = keep.tile([P, N_GROUPS * PACK], BF16, name="ba_sb")
-        bb_sb = keep.tile([P, N_GROUPS * PACK], BF16, name="bb_sb")
-        c_sb = keep.tile([P, N_GROUPS * PACK], BF16, name="c_sb")
-        c32 = keep.tile([P, N_GROUPS * PACK], F32, name="c32")
-        bac = keep.tile([P, N_GROUPS * PACK], F32, name="bac")
+        ba_sb = keep.tile([P, HALVES * PACK], BF16, name="ba_sb")
+        bb_sb = keep.tile([P, HALVES * PACK], BF16, name="bb_sb")
+        c_sb = keep.tile([P, HALVES * PACK], BF16, name="c_sb")
+        c_f32 = keep.tile([P, HALVES * PACK], F32, name="c_f32")
+        ba_c = keep.tile([P, HALVES * PACK], F32, name="ba_c")
         ident = keep.tile([P, P], F32, name="ident")
+        a_scaled, y_t = {}, {}
+        for h in range(HALVES):
+            for chunk in (WIDE, NARROW):
+                users = CHUNKS[chunk][1]
+                a_scaled[h, chunk] = keep.tile([P, PACK * users], F32, name="a_scaled%d%d" % (h, chunk))
+                y_t[h, chunk] = keep.tile([P, PACK * users], F32, name="y_t%d%d" % (h, chunk))
+        y_codes = [keep.tile([P, U], U32, name="y_codes%d" % h, align_bytes=64) for h in range(HALVES)]
+        y_plane = [keep.tile([P, U], U8, name="y_plane%d" % h, align_bytes=64) for h in range(HALVES)]
 
-        x_i32 = x_words.rearrange("g p u t -> g p (u t)").bitcast(I32)
-        xs_i32 = x_scales.bitcast(I32)
-        codes_out = out_1.rearrange("g p u t -> g p (u t)").bitcast(I32)
-        planes_out = out_2.bitcast(I32)
+        x_words_i32 = x_words.rearrange("g p u t -> g p (u t)").bitcast(I32)
+        x_scales_i32 = x_scales.bitcast(I32)
+        out_words_i32 = out_1.rearrange("g p u t -> g p (u t)").bitcast(I32)
+        out_scales_i32 = out_2.bitcast(I32)
+        scale_rows = LIVE_ROWS * (P // QUADRANT)
 
-        def load_piece(i):
-            h, w, g = pieces[i]
+        def load_piece(piece):
+            h, w, g = piece
             rows = weights[w][g * GROUP : (g + 1) * GROUP, h * GROUP : (h + 1) * GROUP]
-            nc.sync.dma_start(out=raw[i][:], in_=rows.rearrange("(p j) n -> p j n", j=PACK))
+            nc.sync.dma_start(out=raw[piece][:], in_=rows.rearrange("(p j) n -> p j n", j=PACK))
 
-        def load_vec(queue, dst, vec):
+        def load_x_wide(g):
+            nc.sync.dma_start(out=x_wide[g][:].bitcast(I32), in_=x_words_i32[g, :, 0:BANK])
+
+        def load_vector(queue, dst, vec):
             queue.dma_start(
                 out=dst[:].rearrange("p (h t) -> p h t", t=PACK),
                 in_=vec.rearrange("(h p t) -> p h t", p=P, t=PACK),
             )
 
-        grouped = {}
+        sorted_w = {}
 
-        def interleave(i, on_vector):
-            if i not in grouped:
-                grouped[i] = stage.tile([P, GROUP * PACK], BF16, name="grouped", align_bytes=64)
-            dst = grouped[i][:].rearrange("p (s t q m j) -> p s q j t m", s=2, t=2, m=2, j=PACK)
-            src = raw[i][:].rearrange("p j (q m s t) -> p s q j t m", m=2, s=2, t=2)
+        def sort_piece(piece, vector_strips):
+            sorted_w[piece] = stage.tile([P, GROUP * PACK], BF16, name="sorted_w", align_bytes=64)
+            dst = sorted_w[piece][:].rearrange("p (s e q d j) -> p s q j e d", s=2, e=2, d=2, j=PACK)
+            src = raw[piece][:].rearrange("p j (q d s e) -> p s q j e d", d=2, s=2, e=2)
+            per_pair = STRIPS // 2
+            cuts = [min(max(vector_strips - s * per_pair, 0), per_pair) for s in range(2)]
             for s in range(2):
-                cut = min(max(V_SHARE[i] * 2 - s * PAIRS, 0), PAIRS)
-                lo, hi = (0, cut) if on_vector else (cut, PAIRS)
-                if lo < hi:
-                    if on_vector:
-                        nc.vector.tensor_copy(out=dst[:, s, lo:hi], in_=src[:, s, lo:hi])
-                    else:
-                        nc.scalar.copy(out=dst[:, s, lo:hi], in_=src[:, s, lo:hi])
+                if cuts[s] > 0:
+                    nc.vector.tensor_copy(out=dst[:, s, : cuts[s]], in_=src[:, s, : cuts[s]])
+            return [(dst[:, s, cuts[s] :], src[:, s, cuts[s] :]) for s in range(2) if cuts[s] < per_pair]
 
-        def quantize_piece(i, halves=(0, 1)):
-            for s in halves:
+        def scalar_copies(strips):
+            for dst, src in strips:
+                nc.scalar.copy(out=dst, in_=src)
+
+        def quantize_piece(piece):
+            for s in range(2):
                 cols = slice(s * 2 * P, (s + 1) * 2 * P)
                 nc.vector.quantize_mx(
-                    out=w_codes[i][:, cols].bitcast(FP8X4),
-                    scales=w_planes[i][:, cols],
-                    in_=grouped[i][:, s * 2 * GROUP : (s + 1) * 2 * GROUP],
+                    out=w_codes[piece][:, cols].bitcast(FP8X4),
+                    scales=w_plane[piece][:, cols],
+                    in_=sorted_w[piece][:, s * 2 * GROUP : (s + 1) * 2 * GROUP],
                 )
-
-        def mx_pass(acc, i, t, chunk):
-            g = pieces[i][2]
-            u0, width = CHUNKS[chunk]
-            cols = slice(t * P, (t + 1) * P)
-            nc.tensor.matmul_mx(
-                out=acc,
-                lhsT=w_codes[i][:, cols].bitcast(FP8X4),
-                lhsT_scale=w_planes[i][:, cols],
-                rhs=x_codes[g][:, u0 : u0 + width].bitcast(FP8X4),
-                rhs_scale=x_plane[:, g * U + u0 : g * U + u0 + width],
-                start=(g == 0),
-                stop=(g == K_GROUPS - 1),
-            )
 
         sums = {}
 
         def take_bank(b):
-            return psum.tile([P, WIDE], F32, name="bank%d" % b)
+            return psum.tile([P, BANK], F32, name="bank%d" % b)
 
-        def mm(i, chunk, banks=None):
-            h, w, g = pieces[i]
+        def mx_pass(piece, chunk, t):
+            h, w, g = piece
+            first, users = CHUNKS[chunk]
+            x_codes = x_wide[g][:] if chunk == WIDE else x_narrow[:, g * users : (g + 1) * users]
+            cols = slice(t * P, (t + 1) * P)
+            nc.tensor.matmul_mx(
+                out=sums[h, w, chunk, t],
+                lhsT=w_codes[piece][:, cols].bitcast(FP8X4),
+                lhsT_scale=w_plane[piece][:, cols],
+                rhs=x_codes.bitcast(FP8X4),
+                rhs_scale=x_plane[:, g * U + first : g * U + first + users],
+                start=(g == 0),
+                stop=(g == K_GROUPS - 1),
+            )
+
+        def open_wide(h, w, banks):
             for t in range(PACK):
-                if g == 0:
-                    sums[h, w, chunk, t] = take_bank(banks[t])[:, 0 : CHUNKS[chunk][1]]
-                mx_pass(sums[h, w, chunk, t], i, t, chunk)
+                sums[h, w, WIDE, t] = take_bank(banks[t])[:]
 
-        def mm_both(i, banks=None):
-            h, w, g = pieces[i]
+        def wide_passes(piece):
             for t in range(PACK):
-                for chunk in (1, 0):
-                    if g == 0:
-                        sums[h, w, chunk, t] = take_bank(banks[chunk][t])[:, 0 : CHUNKS[chunk][1]]
-                    mx_pass(sums[h, w, chunk, t], i, t, chunk)
+                mx_pass(piece, WIDE, t)
 
-        def mm_narrow(h, w, pair, b):
-            first = pieces.index((h, w, 0))
+        def narrow_passes(h, w, pair, b):
             bank = take_bank(b)
             for e in range(2):
                 t = 2 * pair + e
-                sums[h, w, 1, t] = bank[:, e * NARROW : (e + 1) * NARROW]
+                sums[h, w, NARROW, t] = bank[:, e * narrow_users : (e + 1) * narrow_users]
                 for g in range(K_GROUPS):
-                    mx_pass(sums[h, w, 1, t], first + g, t, 1)
+                    mx_pass((h, w, g), NARROW, t)
 
-        scaled = {}
-        y_t = {}
+        def scale_a(h, chunk):
+            users = CHUNKS[chunk][1]
+            for t in range(PACK):
+                col = slice(h * PACK + t, h * PACK + t + 1)
+                nc.scalar.activation(
+                    out=a_scaled[h, chunk][:, t * users : (t + 1) * users],
+                    in_=sums[h, A, chunk, t],
+                    func=ACT.Identity,
+                    scale=c_f32[:, col],
+                    bias=ba_c[:, col],
+                )
 
-        for h in range(N_GROUPS):
-            for chunk in range(2):
-                width = CHUNKS[chunk][1]
-                scaled[h, chunk] = keep.tile([P, PACK * width], F32, name="scaled%d_%d" % (h, chunk))
-                y_t[h, chunk] = keep.tile([P, PACK * width], F32, name="y_t%d_%d" % (h, chunk))
-
-        def scale_a(h, chunk, t):
-            width = CHUNKS[chunk][1]
-            col = slice(h * PACK + t, h * PACK + t + 1)
-            nc.scalar.activation(
-                out=scaled[h, chunk][:, t * width : (t + 1) * width],
-                in_=sums[h, 0, chunk, t],
-                func=ACT.Identity,
-                scale=c32[:, col],
-                bias=bac[:, col],
-            )
-
-        def multiply(h, chunk, t, lo=0, hi=None):
-            width = CHUNKS[chunk][1]
-            hi = hi or width
-            col = slice(h * PACK + t, h * PACK + t + 1)
-            nc.vector.scalar_tensor_tensor(
-                out=y_t[h, chunk][:, t * width + lo : t * width + hi],
-                in0=sums[h, 1, chunk, t][:, lo:hi],
-                scalar=bb_sb[:, col],
-                in1=scaled[h, chunk][:, t * width + lo : t * width + hi],
-                op0=ALU.add,
-                op1=ALU.mult,
-            )
+        def multiply(h, chunk, slots, lo, hi):
+            users = CHUNKS[chunk][1]
+            for t in slots:
+                col = slice(h * PACK + t, h * PACK + t + 1)
+                nc.vector.scalar_tensor_tensor(
+                    out=y_t[h, chunk][:, t * users + lo : t * users + hi],
+                    in0=sums[h, B, chunk, t][:, lo:hi],
+                    scalar=bb_sb[:, col],
+                    in1=a_scaled[h, chunk][:, t * users + lo : t * users + hi],
+                    op0=ALU.add,
+                    op1=ALU.mult,
+                )
 
         turned = {}
 
-        def turn(h, ut, b):
-            chunk = 0 if ut * P < WIDE else 1
-            u0, width = CHUNKS[chunk]
-            bank = take_bank(b)
-            turned[h, ut] = bank
-            for t in range(PACK):
-                at = t * width + ut * P - u0
-                nc.tensor.transpose(bank[:, t * P : (t + 1) * P], y_t[h, chunk][:, at : at + P], ident[:])
+        def turn(h, first_tile, banks):
+            for i, b in enumerate(banks, first_tile):
+                chunk = WIDE if i * P < BANK else NARROW
+                first, users = CHUNKS[chunk]
+                turned[h, i] = take_bank(b)
+                for t in range(PACK):
+                    at = t * users + i * P - first
+                    nc.tensor.transpose(turned[h, i][:, t * P : (t + 1) * P], y_t[h, chunk][:, at : at + P], ident[:])
 
-        def store_y(h, first, count):
-            y_sb = keep.tile([P, count, GROUP], F32, name="y_sb%d_%d" % (h, first))
-            for e in range(count):
+        def store_y(h, first_tile, tiles):
+            y_sb = keep.tile([P, tiles, GROUP], F32, name="y_sb%d%d" % (h, first_tile))
+            for e in range(tiles):
                 nc.scalar.copy(
                     out=y_sb[:, e, :].rearrange("u (m t) -> u m t", t=PACK),
-                    in_=turned[h, first + e][:].rearrange("u (t m) -> u m t", t=PACK),
+                    in_=turned[h, first_tile + e][:].rearrange("u (t m) -> u m t", t=PACK),
                 )
-            rows = out_0[first * P : (first + count) * P, h * GROUP : (h + 1) * GROUP]
-            nc.sync.dma_start(out=rows.rearrange("(e u) n -> u e n", e=count), in_=y_sb[:])
+            rows = out_0[first_tile * P : (first_tile + tiles) * P, h * GROUP : (h + 1) * GROUP]
+            nc.sync.dma_start(out=rows.rearrange("(e u) n -> u e n", e=tiles), in_=y_sb[:])
 
         y_bf = {}
-        y_codes = [keep.tile([P, U], U32, name="y_codes%d" % h, align_bytes=64) for h in range(N_GROUPS)]
-        y_planes = keep.tile([P, U], U8, name="y_planes", align_bytes=64)
 
-        def round_y(h, chunk, on_vector=True):
-            width = CHUNKS[chunk][1]
-            y_bf[h, chunk] = keep.tile([P, PACK * width], BF16, name="y_bf%d_%d" % (h, chunk), align_bytes=64)
-            dst = y_bf[h, chunk][:].rearrange("p (v e t) -> p v t e", t=PACK, e=PACK)
-            src = y_t[h, chunk][:].rearrange("p (t v e) -> p v t e", t=PACK, e=PACK)
-            if on_vector:
-                nc.vector.tensor_copy(out=dst, in_=src)
-            else:
-                nc.scalar.copy(out=dst, in_=src)
+        def round_y(h, chunk, copy):
+            users = CHUNKS[chunk][1]
+            y_bf[h, chunk] = keep.tile([P, PACK * users], BF16, name="y_bf%d%d" % (h, chunk), align_bytes=64)
+            copy(
+                out=y_bf[h, chunk][:].rearrange("p (v e t) -> p v t e", t=PACK, e=4),
+                in_=y_t[h, chunk][:].rearrange("p (t v e) -> p v t e", t=PACK, e=4),
+            )
 
         def quantize_y(h, chunk):
-            u0, width = CHUNKS[chunk]
-            cols = slice(u0, u0 + width)
-            nc.vector.quantize_mx(out=y_codes[h][:, cols].bitcast(FP8X4), scales=y_planes[4 * h :, cols], in_=y_bf[h, chunk][:])
-            nc.sync.dma_start(out=codes_out[h, :, cols], in_=y_codes[h][:, cols].bitcast(I32))
+            first, users = CHUNKS[chunk]
+            cols = slice(first, first + users)
+            nc.vector.quantize_mx(
+                out=y_codes[h][:, cols].bitcast(FP8X4), scales=y_plane[h][:, cols], in_=y_bf[h, chunk][:]
+            )
+            nc.sync.dma_start(out=out_words_i32[h, :, cols], in_=y_codes[h][:, cols].bitcast(I32))
 
-        def store_planes():
-            for q in range(4):
-                queue = nc.sync if q % 2 == 0 else nc.scalar
-                queue.dma_start(
-                    out=planes_out[:, 4 * q : 4 * q + 4, :],
-                    in_=y_planes[32 * q : 32 * q + 4 * N_GROUPS, :].bitcast(I32),
+        def store_plane(h, queues):
+            for r in range(LIVE_ROWS):
+                queues[r % len(queues)].dma_start(
+                    out=out_scales_i32[h, r:scale_rows:LIVE_ROWS, :],
+                    in_=y_plane[h][r:P:QUADRANT, :].bitcast(I32),
                 )
 
         nc.gpsimd.memset(x_plane[:].bitcast(I32), 0)
         make_identity(nc, ident[:])
-        load_vec(nc.scalar, c_sb, c)
-        load_piece(0)
-        nc.sync.dma_start(out=x_codes[0][:].bitcast(I32), in_=x_i32[0])
-        for q in range(4):
+        load_vector(nc.scalar, c_sb, c)
+        load_piece((0, A, 0))
+        load_x_wide(0)
+        for r in range(LIVE_ROWS):
             nc.sync.dma_start(
-                out=x_plane[32 * q : 32 * q + 4, :].bitcast(I32).rearrange("r (g u) -> r g u", g=K_GROUPS),
-                in_=xs_i32[:, 4 * q : 4 * q + 4, :].rearrange("g r u -> r g u"),
+                out=x_plane[r:P:QUADRANT, :].bitcast(I32).rearrange("q (g u) -> q g u", g=K_GROUPS),
+                in_=x_scales_i32[:, r:scale_rows:LIVE_ROWS, :].rearrange("g q u -> q g u"),
             )
-        for kind, n in LOADS:
-            if kind == "w":
-                load_piece(n)
-            elif kind == "x":
-                nc.sync.dma_start(out=x_codes[n][:].bitcast(I32), in_=x_i32[n])
-            else:
-                load_vec(nc.sync, ba_sb, b_a)
-                load_vec(nc.sync, bb_sb, b_b)
+        for g in range(1, K_GROUPS):
+            load_piece((0, A, g))
+            load_x_wide(g)
+        load_vector(nc.sync, ba_sb, b_a)
+        load_piece((0, B, 0))
+        nc.sync.dma_start(
+            out=x_narrow[:].bitcast(I32).rearrange("p (g u) -> p g u", g=K_GROUPS),
+            in_=x_words_i32[:, :, BANK:U].rearrange("g p u -> p g u"),
+        )
+        for g in range(1, K_GROUPS):
+            load_piece((0, B, g))
+        load_vector(nc.sync, bb_sb, b_b)
+        for w in (A, B):
+            for g in range(K_GROUPS):
+                load_piece((1, w, g))
 
-        nc.scalar.activation(out=c32[:], in_=c_sb[:], func=ACT.Identity)
+        nc.scalar.activation(out=c_f32[:], in_=c_sb[:], func=ACT.Identity)
 
-        def both(i):
-            interleave(i, True)
-            interleave(i, False)
+        open_wide(0, A, (0, 1, 2, 3))
+        for g in range(K_GROUPS):
+            scalar_copies(sort_piece((0, A, g), BOTH_FREE))
+            quantize_piece((0, A, g))
+            wide_passes((0, A, g))
+        nc.vector.tensor_tensor(out=ba_c[:], in0=ba_sb[:], in1=c_sb[:], op=ALU.mult)
+        sort_piece((0, B, 0), VECTOR_ALONE)
+        narrow_passes(0, A, 0, 4)
+        narrow_passes(0, A, 1, 5)
+        scale_a(0, WIDE)
 
-        LO, HI = (0, 1, 2, 3), (4, 5, 6, 7)
-        for i in range(3):
-            both(i)
-            quantize_piece(i)
-            mm_both(i, (LO, HI))
-        nc.vector.tensor_tensor(out=bac[:], in0=ba_sb[:], in1=c_sb[:], op=ALU.mult)
-        both(3)
-        for t in range(PACK):
-            scale_a(0, 1, t)
-            scale_a(0, 0, t)
-        quantize_piece(3)
-        mm_both(3, (LO, HI))
-        both(4)
-        quantize_piece(4)
-        mm_both(4)
-        both(5)
-        quantize_piece(5)
-        mm(5, 1)
-        mm(5, 0)
-        both(6)
-        multiply(0, 1, 0)
-        multiply(0, 1, 1)
-        quantize_piece(6)
-        multiply(0, 1, 2)
-        multiply(0, 1, 3)
-        mm(6, 0, HI)
-        multiply(0, 0, 0)
-        multiply(0, 0, 1)
-        both(7)
-        quantize_piece(7)
-        multiply(0, 0, 2)
-        multiply(0, 0, 3)
-        turn(0, 4, 0)
-        turn(0, 5, 1)
-        mm(7, 0)
-        both(8)
-        quantize_piece(8)
-        mm(8, 0)
-        mm_narrow(1, 0, 0, 2)
-        mm_narrow(1, 0, 1, 3)
-        store_y(0, 4, 2)
-        interleave(9, True)
-        for t in range(PACK):
-            scale_a(1, 0, t)
-        interleave(9, False)
-        quantize_piece(9)
-        turn(0, 0, 0)
-        turn(0, 1, 1)
-        mm(9, 0, HI)
-        interleave(10, True)
-        round_y(0, 0)
-        for t in range(PACK):
-            scale_a(1, 1, t)
-        interleave(10, False)
-        quantize_piece(10)
-        mm(10, 0)
-        turn(0, 2, 2)
-        turn(0, 3, 3)
-        both(11)
-        quantize_y(0, 0)
-        quantize_piece(11)
-        mm(11, 0)
+        quantize_piece((0, B, 0))
+        open_wide(0, B, (6, 7, 0, 1))
+        wide_passes((0, B, 0))
+        sort_piece((0, B, 1), VECTOR_ALONE)
+        scale_a(0, NARROW)
+        quantize_piece((0, B, 1))
+        wide_passes((0, B, 1))
+        scalar_copies(sort_piece((0, B, 2), BOTH_FREE))
+        quantize_piece((0, B, 2))
+        wide_passes((0, B, 2))
+        narrow_passes(0, B, 0, 2)
+        narrow_passes(0, B, 1, 3)
+
+        scalar_copies(sort_piece((1, A, 0), BEFORE_PRODUCT))
+        multiply(0, WIDE, (0, 1), 0, BANK)
+        quantize_piece((1, A, 0))
+        multiply(0, WIDE, (2, 3), 0, BANK)
+        open_wide(1, A, (4, 5, 6, 7))
+        wide_passes((1, A, 0))
+        scalar_copies(sort_piece((1, A, 1), SCALAR_ALONE))
+        multiply(0, NARROW, (0, 1), 0, narrow_users)
+        quantize_piece((1, A, 1))
+        multiply(0, NARROW, (2, 3), 0, narrow_users)
+        turn(0, 0, (0, 1))
+        wide_passes((1, A, 1))
+        scalar_copies(sort_piece((1, A, 2), SCALAR_ALONE))
+        quantize_piece((1, A, 2))
+        wide_passes((1, A, 2))
+        narrow_passes(1, A, 0, 2)
+        narrow_passes(1, A, 1, 3)
         store_y(0, 0, 2)
+        sort_piece((1, B, 0), VECTOR_ALONE)
+        scale_a(1, WIDE)
+
+        quantize_piece((1, B, 0))
+        turn(0, 2, (0, 1))
+        open_wide(1, B, (4, 5, 6, 7))
+        wide_passes((1, B, 0))
+        for_scalar = sort_piece((1, B, 1), LAST_BUT_ONE)
+        round_y(0, WIDE, nc.vector.tensor_copy)
+        scale_a(1, NARROW)
+        scalar_copies(for_scalar)
+        quantize_piece((1, B, 1))
+        wide_passes((1, B, 1))
+        turn(0, 4, (2, 3))
+        scalar_copies(sort_piece((1, B, 2), LAST))
+        quantize_y(0, WIDE)
+        quantize_piece((1, B, 2))
+        wide_passes((1, B, 2))
         store_y(0, 2, 2)
-        mm_narrow(1, 1, 0, 0)
-        for t in range(PACK):
-            multiply(1, 0, t, 0, NARROW)
-        turn(1, 0, 2)
-        turn(1, 1, 3)
-        round_y(0, 1, False)
-        for t in range(PACK):
-            multiply(1, 0, t, NARROW, WIDE)
-        store_y(1, 0, 2)
-        turn(1, 2, 4)
-        turn(1, 3, 5)
-        mm_narrow(1, 1, 1, 1)
-        multiply(1, 1, 0)
-        multiply(1, 1, 1)
-        round_y(1, 0)
+        store_y(0, 4, 2)
+
+        narrow_passes(1, B, 0, 0)
+        multiply(1, WIDE, range(PACK), 0, BANK // 2)
+        turn(1, 0, (2, 3))
+        round_y(0, NARROW, nc.scalar.copy)
+        multiply(1, WIDE, range(PACK), BANK // 2, BANK)
+        store_y(1, 0, 1)
+        store_y(1, 1, 1)
+        turn(1, 2, (4, 5))
+        narrow_passes(1, B, 1, 1)
+        quantize_y(0, NARROW)
+        store_plane(0, (nc.sync,))
+        multiply(1, NARROW, (0, 1), 0, narrow_users)
+        round_y(1, WIDE, nc.vector.tensor_copy)
         store_y(1, 2, 2)
-        multiply(1, 1, 2)
-        multiply(1, 1, 3)
-        turn(1, 4, 6)
-        turn(1, 5, 7)
-        quantize_y(0, 1)
-        quantize_y(1, 0)
-        store_y(1, 4, 2)
-        round_y(1, 1)
-        quantize_y(1, 1)
-        store_planes()
+        multiply(1, NARROW, (2, 3), 0, narrow_users)
+        turn(1, 4, (6, 7))
+        quantize_y(1, WIDE)
+        store_y(1, 4, 1)
+        round_y(1, NARROW, nc.vector.tensor_copy)
+        store_y(1, 5, 1)
+        quantize_y(1, NARROW)
+        store_plane(1, (nc.sync, nc.scalar))

@@ -29,19 +29,16 @@ WIDE, NARROW = 0, 1
 CHUNKS = ((0, BANK), (BANK, U - BANK))
 
 STRIPS = 128
-BOTH_FREE = 80
+FIRST_OF_PAIR = 80
+SECOND_OF_PAIR = 48
 VECTOR_ALONE = STRIPS
 SCALAR_ALONE = 0
-BEFORE_PRODUCT = 64
-LAST_BUT_ONE = 112
-LAST = 48
 
 
 def tile_multiplied_user_latents_g6_kernel(
     tc, x_words, x_scales, w_a, b_a, w_b, b_b, c, out_0, out_1, out_2
 ):
     nc = tc.nc
-    weights = (w_a, w_b)
 
     with ExitStack() as ctx:
         keep = ctx.enter_context(tc.tile_pool(name="keep", bufs=1))
@@ -51,8 +48,11 @@ def tile_multiplied_user_latents_g6_kernel(
 
         pieces = [(h, w, g) for h in range(HALVES) for w in (A, B) for g in range(K_GROUPS)]
         raw, w_codes, w_plane = {}, {}, {}
-        for piece in pieces:
-            raw[piece] = keep.tile([P, PACK, GROUP], BF16, name="raw%d%d%d" % piece, align_bytes=64)
+        raw_a = [keep.tile([P, PACK, N], BF16, name="raw_a%d" % g, align_bytes=64) for g in range(K_GROUPS)]
+        for h in range(HALVES):
+            for g in range(K_GROUPS):
+                raw[h, A, g] = raw_a[g][:, :, h * GROUP : (h + 1) * GROUP]
+                raw[h, B, g] = keep.tile([P, PACK, GROUP], BF16, name="raw_b%d%d" % (h, g), align_bytes=64)[:]
         for piece in pieces:
             w_codes[piece] = keep.tile([P, GROUP], U32, name="w_codes%d%d%d" % piece, align_bytes=64)
         for piece in pieces:
@@ -82,13 +82,25 @@ def tile_multiplied_user_latents_g6_kernel(
         out_scales_i32 = out_2.bitcast(I32)
         scale_rows = LIVE_ROWS * (P // QUADRANT)
 
-        def load_piece(piece):
-            h, w, g = piece
-            rows = weights[w][g * GROUP : (g + 1) * GROUP, h * GROUP : (h + 1) * GROUP]
-            nc.sync.dma_start(out=raw[piece][:], in_=rows.rearrange("(p j) n -> p j n", j=PACK))
+        def load_rows(dst, rows):
+            nc.sync.dma_start(out=dst, in_=rows.rearrange("(p j) n -> p j n", j=PACK))
+
+        def load_a(g):
+            load_rows(raw_a[g][:], w_a[g * GROUP : (g + 1) * GROUP, :])
+
+        def load_b(h, g):
+            load_rows(raw[h, B, g], w_b[g * GROUP : (g + 1) * GROUP, h * GROUP : (h + 1) * GROUP])
 
         def load_x_wide(g):
             nc.sync.dma_start(out=x_wide[g][:].bitcast(I32), in_=x_words_i32[g, :, 0:BANK])
+
+        def load_x_scales(queue, g_first, g_end):
+            for r in range(LIVE_ROWS):
+                live = x_plane[r:P:QUADRANT, g_first * U : g_end * U]
+                queue.dma_start(
+                    out=live.bitcast(I32).rearrange("q (g u) -> q g u", g=g_end - g_first),
+                    in_=x_scales_i32[g_first:g_end, r:scale_rows:LIVE_ROWS, :].rearrange("g q u -> q g u"),
+                )
 
         def load_vector(queue, dst, vec):
             queue.dma_start(
@@ -101,7 +113,7 @@ def tile_multiplied_user_latents_g6_kernel(
         def sort_piece(piece, vector_strips):
             sorted_w[piece] = stage.tile([P, GROUP * PACK], BF16, name="sorted_w", align_bytes=64)
             dst = sorted_w[piece][:].rearrange("p (s e q d j) -> p s q j e d", s=2, e=2, d=2, j=PACK)
-            src = raw[piece][:].rearrange("p j (q d s e) -> p s q j e d", d=2, s=2, e=2)
+            src = raw[piece].rearrange("p j (q d s e) -> p s q j e d", d=2, s=2, e=2)
             per_pair = STRIPS // 2
             cuts = [min(max(vector_strips - s * per_pair, 0), per_pair) for s in range(2)]
             for s in range(2):
@@ -230,115 +242,96 @@ def tile_multiplied_user_latents_g6_kernel(
                 )
 
         nc.gpsimd.memset(x_plane[:].bitcast(I32), 0)
-        make_identity(nc, ident[:])
         load_vector(nc.scalar, c_sb, c)
-        load_piece((0, A, 0))
+        load_a(0)
         load_x_wide(0)
-        for r in range(LIVE_ROWS):
-            nc.sync.dma_start(
-                out=x_plane[r:P:QUADRANT, :].bitcast(I32).rearrange("q (g u) -> q g u", g=K_GROUPS),
-                in_=x_scales_i32[:, r:scale_rows:LIVE_ROWS, :].rearrange("g q u -> q g u"),
-            )
+        load_x_scales(nc.sync, 0, 1)
+        load_x_scales(nc.gpsimd, 1, K_GROUPS)
+        make_identity(nc, ident[:])
         for g in range(1, K_GROUPS):
-            load_piece((0, A, g))
+            load_a(g)
             load_x_wide(g)
         load_vector(nc.sync, ba_sb, b_a)
-        load_piece((0, B, 0))
         nc.sync.dma_start(
             out=x_narrow[:].bitcast(I32).rearrange("p (g u) -> p g u", g=K_GROUPS),
             in_=x_words_i32[:, :, BANK:U].rearrange("g p u -> p g u"),
         )
-        for g in range(1, K_GROUPS):
-            load_piece((0, B, g))
+        for g in range(K_GROUPS):
+            load_b(0, g)
         load_vector(nc.sync, bb_sb, b_b)
-        for w in (A, B):
-            for g in range(K_GROUPS):
-                load_piece((1, w, g))
+        for g in range(K_GROUPS):
+            load_b(1, g)
 
         nc.scalar.activation(out=c_f32[:], in_=c_sb[:], func=ACT.Identity)
 
         open_wide(0, A, (0, 1, 2, 3))
+        open_wide(1, A, (4, 5, 6, 7))
         for g in range(K_GROUPS):
-            scalar_copies(sort_piece((0, A, g), BOTH_FREE))
+            scalar_copies(sort_piece((0, A, g), FIRST_OF_PAIR))
             quantize_piece((0, A, g))
             wide_passes((0, A, g))
-        nc.vector.tensor_tensor(out=ba_c[:], in0=ba_sb[:], in1=c_sb[:], op=ALU.mult)
-        sort_piece((0, B, 0), VECTOR_ALONE)
-        narrow_passes(0, A, 0, 4)
-        narrow_passes(0, A, 1, 5)
+            if g == K_GROUPS - 1:
+                nc.vector.tensor_tensor(out=ba_c[:], in0=ba_sb[:], in1=c_sb[:], op=ALU.mult)
+            scalar_copies(sort_piece((1, A, g), SECOND_OF_PAIR))
+            quantize_piece((1, A, g))
+            wide_passes((1, A, g))
+
         scale_a(0, WIDE)
-
-        quantize_piece((0, B, 0))
-        open_wide(0, B, (6, 7, 0, 1))
-        wide_passes((0, B, 0))
-        sort_piece((0, B, 1), VECTOR_ALONE)
-        scale_a(0, NARROW)
-        quantize_piece((0, B, 1))
-        wide_passes((0, B, 1))
-        scalar_copies(sort_piece((0, B, 2), BOTH_FREE))
-        quantize_piece((0, B, 2))
-        wide_passes((0, B, 2))
-        narrow_passes(0, B, 0, 2)
-        narrow_passes(0, B, 1, 3)
-
-        scalar_copies(sort_piece((1, A, 0), BEFORE_PRODUCT))
-        multiply(0, WIDE, (0, 1), 0, BANK)
-        quantize_piece((1, A, 0))
-        multiply(0, WIDE, (2, 3), 0, BANK)
-        open_wide(1, A, (4, 5, 6, 7))
-        wide_passes((1, A, 0))
-        scalar_copies(sort_piece((1, A, 1), SCALAR_ALONE))
-        multiply(0, NARROW, (0, 1), 0, narrow_users)
-        quantize_piece((1, A, 1))
-        multiply(0, NARROW, (2, 3), 0, narrow_users)
-        turn(0, 0, (0, 1))
-        wide_passes((1, A, 1))
-        scalar_copies(sort_piece((1, A, 2), SCALAR_ALONE))
-        quantize_piece((1, A, 2))
-        wide_passes((1, A, 2))
+        narrow_passes(0, A, 0, 0)
+        narrow_passes(0, A, 1, 1)
         narrow_passes(1, A, 0, 2)
         narrow_passes(1, A, 1, 3)
-        store_y(0, 0, 2)
-        sort_piece((1, B, 0), VECTOR_ALONE)
         scale_a(1, WIDE)
-
-        quantize_piece((1, B, 0))
-        turn(0, 2, (0, 1))
-        open_wide(1, B, (4, 5, 6, 7))
-        wide_passes((1, B, 0))
-        for_scalar = sort_piece((1, B, 1), LAST_BUT_ONE)
-        round_y(0, WIDE, nc.vector.tensor_copy)
+        scale_a(0, NARROW)
         scale_a(1, NARROW)
-        scalar_copies(for_scalar)
+        open_wide(0, B, (4, 5, 6, 7))
+        for g in range(K_GROUPS):
+            sort_piece((0, B, g), VECTOR_ALONE)
+            quantize_piece((0, B, g))
+            wide_passes((0, B, g))
+        narrow_passes(0, B, 0, 0)
+        narrow_passes(0, B, 1, 1)
+
+        sort_piece((1, B, 0), VECTOR_ALONE)
+        multiply(0, WIDE, (0, 1), 0, BANK)
+        quantize_piece((1, B, 0))
+        multiply(0, WIDE, (2, 3), 0, BANK)
+        open_wide(1, B, (2, 3, 4, 5))
+        wide_passes((1, B, 0))
+        turn(0, 0, (6, 7))
+        scalar_copies(sort_piece((1, B, 1), SCALAR_ALONE))
         quantize_piece((1, B, 1))
         wide_passes((1, B, 1))
-        turn(0, 4, (2, 3))
-        scalar_copies(sort_piece((1, B, 2), LAST))
-        quantize_y(0, WIDE)
+        scalar_copies(sort_piece((1, B, 2), SCALAR_ALONE))
+        multiply(0, NARROW, range(PACK), 0, narrow_users)
         quantize_piece((1, B, 2))
+        store_y(0, 0, 2)
+        turn(0, 2, (0, 1))
         wide_passes((1, B, 2))
-        store_y(0, 2, 2)
-        store_y(0, 4, 2)
-
-        narrow_passes(1, B, 0, 0)
-        multiply(1, WIDE, range(PACK), 0, BANK // 2)
-        turn(1, 0, (2, 3))
         round_y(0, NARROW, nc.scalar.copy)
-        multiply(1, WIDE, range(PACK), BANK // 2, BANK)
-        store_y(1, 0, 1)
-        store_y(1, 1, 1)
-        turn(1, 2, (4, 5))
-        narrow_passes(1, B, 1, 1)
+        round_y(0, WIDE, nc.vector.tensor_copy)
         quantize_y(0, NARROW)
+        turn(0, 4, (6, 7))
+        store_y(0, 2, 2)
+
+        multiply(1, WIDE, range(PACK), 0, BANK // 2)
+        quantize_y(0, WIDE)
         store_plane(0, (nc.sync,))
+        turn(1, 0, (0, 1))
+        store_y(0, 4, 2)
+        multiply(1, WIDE, range(PACK), BANK // 2, BANK)
+        narrow_passes(1, B, 0, 6)
+        store_y(1, 0, 2)
+        turn(1, 2, (2, 3))
+        narrow_passes(1, B, 1, 7)
         multiply(1, NARROW, (0, 1), 0, narrow_users)
         round_y(1, WIDE, nc.vector.tensor_copy)
         store_y(1, 2, 2)
         multiply(1, NARROW, (2, 3), 0, narrow_users)
-        turn(1, 4, (6, 7))
+        turn(1, 4, (4, 5))
         quantize_y(1, WIDE)
-        store_y(1, 4, 1)
         round_y(1, NARROW, nc.vector.tensor_copy)
+        store_y(1, 4, 1)
         store_y(1, 5, 1)
         quantize_y(1, NARROW)
         store_plane(1, (nc.sync, nc.scalar))

@@ -60,7 +60,10 @@ def tile_multiplied_user_latents_g6_kernel(
         narrow_users = CHUNKS[NARROW][1]
         x_wide = [keep.tile([P, BANK], U32, name="x_wide%d" % g, align_bytes=64) for g in range(K_GROUPS)]
         x_narrow = keep.tile([P, K_GROUPS * narrow_users], U32, name="x_narrow", align_bytes=64)
-        x_plane = keep.tile([P, K_GROUPS * U], U8, name="x_plane", align_bytes=64)
+        early_groups = K_GROUPS - 1
+        x_plane_early = keep.tile([P, early_groups * U], U8, name="x_plane_early", align_bytes=64)
+        x_plane_late = keep.tile([P, U], U8, name="x_plane_late", align_bytes=64)
+        x_plane = [x_plane_early[:, g * U : (g + 1) * U] for g in range(early_groups)] + [x_plane_late[:]]
         ba_sb = keep.tile([P, HALVES * PACK], BF16, name="ba_sb")
         bb_sb = keep.tile([P, HALVES * PACK], BF16, name="bb_sb")
         c_sb = keep.tile([P, HALVES * PACK], BF16, name="c_sb")
@@ -94,11 +97,10 @@ def tile_multiplied_user_latents_g6_kernel(
         def load_x_wide(g):
             nc.sync.dma_start(out=x_wide[g][:].bitcast(I32), in_=x_words_i32[g, :, 0:BANK])
 
-        def load_x_scales(queue, g_first, g_end):
+        def load_x_scales(planes, g_first, g_end):
             for r in range(LIVE_ROWS):
-                live = x_plane[r:P:QUADRANT, g_first * U : g_end * U]
-                queue.dma_start(
-                    out=live.bitcast(I32).rearrange("q (g u) -> q g u", g=g_end - g_first),
+                nc.sync.dma_start(
+                    out=planes[r:P:QUADRANT, :].bitcast(I32).rearrange("q (g u) -> q g u", g=g_end - g_first),
                     in_=x_scales_i32[g_first:g_end, r:scale_rows:LIVE_ROWS, :].rearrange("g q u -> q g u"),
                 )
 
@@ -149,7 +151,7 @@ def tile_multiplied_user_latents_g6_kernel(
                 lhsT=w_codes[piece][:, cols].bitcast(FP8X4),
                 lhsT_scale=w_plane[piece][:, cols],
                 rhs=x_codes.bitcast(FP8X4),
-                rhs_scale=x_plane[:, g * U + first : g * U + first + users],
+                rhs_scale=x_plane[g][:, first : first + users],
                 start=(g == 0),
                 stop=(g == K_GROUPS - 1),
             )
@@ -241,22 +243,24 @@ def tile_multiplied_user_latents_g6_kernel(
                     in_=y_plane[h][r:P:QUADRANT, :].bitcast(I32),
                 )
 
-        nc.gpsimd.memset(x_plane[:].bitcast(I32), 0)
+        nc.gpsimd.memset(x_plane_early[:].bitcast(I32), 0)
+        nc.gpsimd.memset(x_plane_late[:].bitcast(I32), 0)
+        make_identity(nc, ident[:])
         load_vector(nc.scalar, c_sb, c)
         load_a(0)
         load_x_wide(0)
-        load_x_scales(nc.sync, 0, 1)
-        load_x_scales(nc.gpsimd, 1, K_GROUPS)
-        make_identity(nc, ident[:])
+        load_x_scales(x_plane_early, 0, early_groups)
         for g in range(1, K_GROUPS):
             load_a(g)
             load_x_wide(g)
+        load_x_scales(x_plane_late, early_groups, K_GROUPS)
         load_vector(nc.sync, ba_sb, b_a)
+        load_b(0, 0)
         nc.sync.dma_start(
             out=x_narrow[:].bitcast(I32).rearrange("p (g u) -> p g u", g=K_GROUPS),
             in_=x_words_i32[:, :, BANK:U].rearrange("g p u -> p g u"),
         )
-        for g in range(K_GROUPS):
+        for g in range(1, K_GROUPS):
             load_b(0, g)
         load_vector(nc.sync, bb_sb, b_b)
         for g in range(K_GROUPS):

from contextlib import ExitStack

import concourse.mybir as mybir
from concourse.masks import make_identity

U, D, N = 768, 1536, 1024
FLOPS = 2 * 2 * U * D * N

F32 = mybir.dt.float32
BF16 = mybir.dt.bfloat16
I32 = mybir.dt.int32
U32 = mybir.dt.uint32
U8 = mybir.dt.uint8
FP8X4 = mybir.dt.float8_e4m3fn_x4
ACT = mybir.ActivationFunctionType
ALU = mybir.AluOpType

P = 128
PACK = 4
GROUP = P * PACK
K_GROUPS = D // GROUP
HALVES = N // GROUP
BANK = 512
QUADRANT = 32
LIVE_ROWS = 4
A, B = 0, 1

WIDE, NARROW = 0, 1
CHUNKS = ((0, BANK), (BANK, U - BANK))

STRIPS = 128
FIRST_OF_PAIR = 80
SECOND_OF_PAIR = 48
VECTOR_ALONE = STRIPS
SCALAR_ALONE = 0


def tile_multiplied_user_latents_g6_kernel(
    tc, x_words, x_scales, w_a, b_a, w_b, b_b, c, out_0, out_1, out_2
):
    nc = tc.nc

    with ExitStack() as ctx:
        keep = ctx.enter_context(tc.tile_pool(name="keep", bufs=1))
        stage = ctx.enter_context(tc.tile_pool(name="stage", bufs=4))
        psum = ctx.enter_context(tc.psum_pool(name="psum", bufs=1))
        ctx.enter_context(tc.manual_schedule())

        pieces = [(h, w, g) for h in range(HALVES) for w in (A, B) for g in range(K_GROUPS)]
        raw, w_codes, w_plane = {}, {}, {}
        raw_a = [keep.tile([P, PACK, N], BF16, name="raw_a%d" % g, align_bytes=64) for g in range(K_GROUPS)]
        for h in range(HALVES):
            for g in range(K_GROUPS):
                raw[h, A, g] = raw_a[g][:, :, h * GROUP : (h + 1) * GROUP]
                raw[h, B, g] = keep.tile([P, PACK, GROUP], BF16, name="raw_b%d%d" % (h, g), align_bytes=64)[:]
        for piece in pieces:
            w_codes[piece] = keep.tile([P, GROUP], U32, name="w_codes%d%d%d" % piece, align_bytes=64)
        for piece in pieces:
            w_plane[piece] = keep.tile([P, GROUP], U8, name="w_plane%d%d%d" % piece, align_bytes=64)
        narrow_users = CHUNKS[NARROW][1]
        x_wide = [keep.tile([P, BANK], U32, name="x_wide%d" % g, align_bytes=64) for g in range(K_GROUPS)]
        x_narrow = keep.tile([P, K_GROUPS * narrow_users], U32, name="x_narrow", align_bytes=64)
        early_groups = K_GROUPS - 1
        x_plane_early = keep.tile([P, early_groups * U], U8, name="x_plane_early", align_bytes=64)
        x_plane_late = keep.tile([P, U], U8, name="x_plane_late", align_bytes=64)
        x_plane = [x_plane_early[:, g * U : (g + 1) * U] for g in range(early_groups)] + [x_plane_late[:]]
        ba_sb = keep.tile([P, HALVES * PACK], BF16, name="ba_sb")
        bb_sb = keep.tile([P, HALVES * PACK], BF16, name="bb_sb")
        c_sb = keep.tile([P, HALVES * PACK], BF16, name="c_sb")
        c_f32 = keep.tile([P, HALVES * PACK], F32, name="c_f32")
        ba_c = keep.tile([P, HALVES * PACK], F32, name="ba_c")
        ident = keep.tile([P, P], F32, name="ident")
        a_scaled, y_t = {}, {}
        for h in range(HALVES):
            for chunk in (WIDE, NARROW):
                users = CHUNKS[chunk][1]
                a_scaled[h, chunk] = keep.tile([P, PACK * users], F32, name="a_scaled%d%d" % (h, chunk))
                y_t[h, chunk] = keep.tile([P, PACK * users], F32, name="y_t%d%d" % (h, chunk))
        y_codes = [keep.tile([P, U], U32, name="y_codes%d" % h, align_bytes=64) for h in range(HALVES)]
        y_plane = [keep.tile([P, U], U8, name="y_plane%d" % h, align_bytes=64) for h in range(HALVES)]

        x_words_i32 = x_words.rearrange("g p u t -> g p (u t)").bitcast(I32)
        x_scales_i32 = x_scales.bitcast(I32)
        out_words_i32 = out_1.rearrange("g p u t -> g p (u t)").bitcast(I32)
        out_scales_i32 = out_2.bitcast(I32)
        scale_rows = LIVE_ROWS * (P // QUADRANT)

        def load_rows(dst, rows):
            nc.sync.dma_start(out=dst, in_=rows.rearrange("(p j) n -> p j n", j=PACK))

        def load_a(g):
            load_rows(raw_a[g][:], w_a[g * GROUP : (g + 1) * GROUP, :])

        def load_b(h, g):
            load_rows(raw[h, B, g], w_b[g * GROUP : (g + 1) * GROUP, h * GROUP : (h + 1) * GROUP])

        def load_x_wide(g):
            nc.sync.dma_start(out=x_wide[g][:].bitcast(I32), in_=x_words_i32[g, :, 0:BANK])

        def load_x_scales(planes, g_first, g_end):
            for r in range(LIVE_ROWS):
                nc.sync.dma_start(
                    out=planes[r:P:QUADRANT, :].bitcast(I32).rearrange("q (g u) -> q g u", g=g_end - g_first),
                    in_=x_scales_i32[g_first:g_end, r:scale_rows:LIVE_ROWS, :].rearrange("g q u -> q g u"),
                )

        def load_vector(queue, dst, vec):
            queue.dma_start(
                out=dst[:].rearrange("p (h t) -> p h t", t=PACK),
                in_=vec.rearrange("(h p t) -> p h t", p=P, t=PACK),
            )

        sorted_w = {}

        def sort_piece(piece, vector_strips):
            sorted_w[piece] = stage.tile([P, GROUP * PACK], BF16, name="sorted_w", align_bytes=64)
            dst = sorted_w[piece][:].rearrange("p (s e q d j) -> p s q j e d", s=2, e=2, d=2, j=PACK)
            src = raw[piece].rearrange("p j (q d s e) -> p s q j e d", d=2, s=2, e=2)
            per_pair = STRIPS // 2
            cuts = [min(max(vector_strips - s * per_pair, 0), per_pair) for s in range(2)]
            for s in range(2):
                if cuts[s] > 0:
                    nc.vector.tensor_copy(out=dst[:, s, : cuts[s]], in_=src[:, s, : cuts[s]])
            return [(dst[:, s, cuts[s] :], src[:, s, cuts[s] :]) for s in range(2) if cuts[s] < per_pair]

        def scalar_copies(strips):
            for dst, src in strips:
                nc.scalar.copy(out=dst, in_=src)

        def quantize_piece(piece):
            for s in range(2):
                cols = slice(s * 2 * P, (s + 1) * 2 * P)
                nc.vector.quantize_mx(
                    out=w_codes[piece][:, cols].bitcast(FP8X4),
                    scales=w_plane[piece][:, cols],
                    in_=sorted_w[piece][:, s * 2 * GROUP : (s + 1) * 2 * GROUP],
                )

        sums = {}

        def take_bank(b):
            return psum.tile([P, BANK], F32, name="bank%d" % b)

        def mx_pass(piece, chunk, t):
            h, w, g = piece
            first, users = CHUNKS[chunk]
            x_codes = x_wide[g][:] if chunk == WIDE else x_narrow[:, g * users : (g + 1) * users]
            cols = slice(t * P, (t + 1) * P)
            nc.tensor.matmul_mx(
                out=sums[h, w, chunk, t],
                lhsT=w_codes[piece][:, cols].bitcast(FP8X4),
                lhsT_scale=w_plane[piece][:, cols],
                rhs=x_codes.bitcast(FP8X4),
                rhs_scale=x_plane[g][:, first : first + users],
                start=(g == 0),
                stop=(g == K_GROUPS - 1),
            )

        def open_wide(h, w, banks):
            for t in range(PACK):
                sums[h, w, WIDE, t] = take_bank(banks[t])[:]

        def wide_passes(piece):
            for t in range(PACK):
                mx_pass(piece, WIDE, t)

        def narrow_passes(h, w, pair, b):
            bank = take_bank(b)
            for e in range(2):
                t = 2 * pair + e
                sums[h, w, NARROW, t] = bank[:, e * narrow_users : (e + 1) * narrow_users]
                for g in range(K_GROUPS):
                    mx_pass((h, w, g), NARROW, t)

        def scale_a(h, chunk):
            users = CHUNKS[chunk][1]
            for t in range(PACK):
                col = slice(h * PACK + t, h * PACK + t + 1)
                nc.scalar.activation(
                    out=a_scaled[h, chunk][:, t * users : (t + 1) * users],
                    in_=sums[h, A, chunk, t],
                    func=ACT.Identity,
                    scale=c_f32[:, col],
                    bias=ba_c[:, col],
                )

        def multiply(h, chunk, slots, lo, hi):
            users = CHUNKS[chunk][1]
            for t in slots:
                col = slice(h * PACK + t, h * PACK + t + 1)
                nc.vector.scalar_tensor_tensor(
                    out=y_t[h, chunk][:, t * users + lo : t * users + hi],
                    in0=sums[h, B, chunk, t][:, lo:hi],
                    scalar=bb_sb[:, col],
                    in1=a_scaled[h, chunk][:, t * users + lo : t * users + hi],
                    op0=ALU.add,
                    op1=ALU.mult,
                )

        turned = {}

        def turn(h, first_tile, banks):
            for i, b in enumerate(banks, first_tile):
                chunk = WIDE if i * P < BANK else NARROW
                first, users = CHUNKS[chunk]
                turned[h, i] = take_bank(b)
                for t in range(PACK):
                    at = t * users + i * P - first
                    nc.tensor.transpose(turned[h, i][:, t * P : (t + 1) * P], y_t[h, chunk][:, at : at + P], ident[:])

        def store_y(h, first_tile, tiles):
            y_sb = keep.tile([P, tiles, GROUP], F32, name="y_sb%d%d" % (h, first_tile))
            for e in range(tiles):
                nc.scalar.copy(
                    out=y_sb[:, e, :].rearrange("u (m t) -> u m t", t=PACK),
                    in_=turned[h, first_tile + e][:].rearrange("u (t m) -> u m t", t=PACK),
                )
            rows = out_0[first_tile * P : (first_tile + tiles) * P, h * GROUP : (h + 1) * GROUP]
            nc.sync.dma_start(out=rows.rearrange("(e u) n -> u e n", e=tiles), in_=y_sb[:])

        y_bf = {}

        def round_y(h, chunk, copy):
            users = CHUNKS[chunk][1]
            y_bf[h, chunk] = keep.tile([P, PACK * users], BF16, name="y_bf%d%d" % (h, chunk), align_bytes=64)
            copy(
                out=y_bf[h, chunk][:].rearrange("p (v e t) -> p v t e", t=PACK, e=4),
                in_=y_t[h, chunk][:].rearrange("p (t v e) -> p v t e", t=PACK, e=4),
            )

        def quantize_y(h, chunk):
            first, users = CHUNKS[chunk]
            cols = slice(first, first + users)
            nc.vector.quantize_mx(
                out=y_codes[h][:, cols].bitcast(FP8X4), scales=y_plane[h][:, cols], in_=y_bf[h, chunk][:]
            )
            nc.sync.dma_start(out=out_words_i32[h, :, cols], in_=y_codes[h][:, cols].bitcast(I32))

        def store_plane(h, queues):
            for r in range(LIVE_ROWS):
                queues[r % len(queues)].dma_start(
                    out=out_scales_i32[h, r:scale_rows:LIVE_ROWS, :],
                    in_=y_plane[h][r:P:QUADRANT, :].bitcast(I32),
                )

        nc.gpsimd.memset(x_plane_early[:].bitcast(I32), 0)
        nc.gpsimd.memset(x_plane_late[:].bitcast(I32), 0)
        make_identity(nc, ident[:])
        load_vector(nc.scalar, c_sb, c)
        load_a(0)
        load_x_wide(0)
        load_x_scales(x_plane_early, 0, early_groups)
        for g in range(1, K_GROUPS):
            load_a(g)
            load_x_wide(g)
        load_x_scales(x_plane_late, early_groups, K_GROUPS)
        load_vector(nc.sync, ba_sb, b_a)
        load_b(0, 0)
        nc.sync.dma_start(
            out=x_narrow[:].bitcast(I32).rearrange("p (g u) -> p g u", g=K_GROUPS),
            in_=x_words_i32[:, :, BANK:U].rearrange("g p u -> p g u"),
        )
        for g in range(1, K_GROUPS):
            load_b(0, g)
        load_vector(nc.sync, bb_sb, b_b)
        for g in range(K_GROUPS):
            load_b(1, g)

        nc.scalar.activation(out=c_f32[:], in_=c_sb[:], func=ACT.Identity)

        open_wide(0, A, (0, 1, 2, 3))
        open_wide(1, A, (4, 5, 6, 7))
        for g in range(K_GROUPS):
            scalar_copies(sort_piece((0, A, g), FIRST_OF_PAIR))
            quantize_piece((0, A, g))
            wide_passes((0, A, g))
            if g == K_GROUPS - 1:
                nc.vector.tensor_tensor(out=ba_c[:], in0=ba_sb[:], in1=c_sb[:], op=ALU.mult)
            scalar_copies(sort_piece((1, A, g), SECOND_OF_PAIR))
            quantize_piece((1, A, g))
            wide_passes((1, A, g))

        scale_a(0, WIDE)
        narrow_passes(0, A, 0, 0)
        narrow_passes(0, A, 1, 1)
        narrow_passes(1, A, 0, 2)
        narrow_passes(1, A, 1, 3)
        scale_a(1, WIDE)
        scale_a(0, NARROW)
        scale_a(1, NARROW)
        open_wide(0, B, (4, 5, 6, 7))
        for g in range(K_GROUPS):
            sort_piece((0, B, g), VECTOR_ALONE)
            quantize_piece((0, B, g))
            wide_passes((0, B, g))
        narrow_passes(0, B, 0, 0)
        narrow_passes(0, B, 1, 1)

        sort_piece((1, B, 0), VECTOR_ALONE)
        multiply(0, WIDE, (0, 1), 0, BANK)
        quantize_piece((1, B, 0))
        multiply(0, WIDE, (2, 3), 0, BANK)
        open_wide(1, B, (2, 3, 4, 5))
        wide_passes((1, B, 0))
        turn(0, 0, (6, 7))
        scalar_copies(sort_piece((1, B, 1), SCALAR_ALONE))
        quantize_piece((1, B, 1))
        wide_passes((1, B, 1))
        scalar_copies(sort_piece((1, B, 2), SCALAR_ALONE))
        multiply(0, NARROW, range(PACK), 0, narrow_users)
        quantize_piece((1, B, 2))
        store_y(0, 0, 2)
        turn(0, 2, (0, 1))
        wide_passes((1, B, 2))
        round_y(0, NARROW, nc.scalar.copy)
        round_y(0, WIDE, nc.vector.tensor_copy)
        quantize_y(0, NARROW)
        turn(0, 4, (6, 7))
        store_y(0, 2, 2)

        multiply(1, WIDE, range(PACK), 0, BANK // 2)
        quantize_y(0, WIDE)
        store_plane(0, (nc.sync,))
        turn(1, 0, (0, 1))
        store_y(0, 4, 2)
        multiply(1, WIDE, range(PACK), BANK // 2, BANK)
        narrow_passes(1, B, 0, 6)
        store_y(1, 0, 2)
        turn(1, 2, (2, 3))
        narrow_passes(1, B, 1, 7)
        multiply(1, NARROW, (0, 1), 0, narrow_users)
        round_y(1, WIDE, nc.vector.tensor_copy)
        store_y(1, 2, 2)
        multiply(1, NARROW, (2, 3), 0, narrow_users)
        turn(1, 4, (4, 5))
        quantize_y(1, WIDE)
        round_y(1, NARROW, nc.vector.tensor_copy)
        store_y(1, 4, 1)
        store_y(1, 5, 1)
        quantize_y(1, NARROW)
        store_plane(1, (nc.sync, nc.scalar))
